import numpy as np, ml_dtypes
CORES = [8,136,40,168]
N = 4
BF = ml_dtypes.bfloat16
def gentries(a):
    return np.ascontiguousarray(a.reshape(8, 16, -1).transpose(0, 2, 1)).reshape(8, -1)
def gtable(e):
    e = np.asarray(e); return np.ascontiguousarray(e.reshape(8, -1, 16).transpose(0, 2, 1)).reshape(128, -1).astype(np.int32)
W, F, FC, LM, CAP, TS, LB, RO = 1664, 256, 384, 64, 48, 1024, 2, 3
WT = 255 - 14 * np.arange(16)
M = 8
def pick(t, ix):
    return np.take_along_axis(t, ix[:, :, None, :], 3)
def letters(rng, uneven):
    C = W // M; A = C // 4; hc = (A // 2) * 4; hw = hc * M
    if uneven:
        v = (np.floor(np.exp2(8 * rng.random((N, 8, 1, C))) * rng.random((N, 8, 16, C))) * (rng.random((N, 8, 1, C)) > 0.0625)).astype(np.int64)
        q = (np.floor(np.exp2(8 * rng.random((N, 8, 1, W))) * rng.random((N, 8, 16, W))) * (rng.random((N, 8, 1, W)) > 0.0625)).astype(np.int64)
    else:
        v = rng.integers(0, 256, (N, 8, 16, C)); q = rng.integers(0, 256, (N, 8, 16, W))
    base = rng.integers(0, C, (N, 8, A, 16)); base[:, :, :A // 2] %= hc
    alt = rng.integers(0, C, (N, 8, C, 16)); alt[:, :, :hc] %= hc
    seq = np.repeat(base, 4, axis=2); seq = np.where(rng.random(seq.shape) < 0.08, alt, seq)
    blk = np.repeat(np.add.accumulate((rng.random((N, 8, A, 16)) < 0.6).astype(np.int64), axis=3), 4 * M, axis=2)
    loose = np.take_along_axis(rng.random((N, 8, W, 17)), blk, 3) < rng.choice(np.array([0.15, 0.3, 0.5]), (N, 8, 1, 1))
    order = np.argsort(blk + np.where(loose, rng.random(blk.shape), 0.0625 * np.arange(16)), axis=3)
    mem = np.repeat(rng.integers(0, M, (N, 8, A, 16)), 4 * M, axis=2)
    mem = np.where(rng.random(mem.shape) < rng.choice(np.array([0.02, 0.06, 0.15, 0.4]), (N, 8, 1, 1)), rng.integers(0, M, mem.shape), mem)
    kid = np.take_along_axis(np.repeat(seq, M, axis=2) * M + mem, order, 3)
    v[:, :, :, :hc] = v[:1, :, :, :hc].copy(); q[:, :, :, :hw] = q[:1, :, :, :hw].copy(); kid[:, :, :hw] = kid[:1, :, :hw].copy()
    return np.repeat(v, M, axis=3), q, kid
def front(rng, skew):
    A = W // (4 * M)
    st = rng.random((N, 8, F)) < rng.choice(np.array([0.3, 0.5, 0.8]), (N, 8, 1)); st[:, :, 0] = True
    st = st.astype(np.int64); sid = np.add.accumulate(st, axis=2) - 1
    fam = (A * rng.random((N, 8, F)) ** (3 if skew else 1)).astype(np.int64)
    fam = np.take_along_axis(np.where(rng.random(fam.shape) < 0.7, fam % (A // 2), fam), sid, 2)
    c = fam * 4 + rng.integers(0, 4, fam.shape); m = rng.integers(0, M, fam.shape)
    o = np.argsort(sid + 0.99 * rng.random(fam.shape), axis=2)
    mv = np.where(rng.random(fam.shape) < 0.3, np.take_along_axis(m, o, 2), rng.integers(0, M, fam.shape))
    fv = np.take_along_axis(c, o, 2) * M + mv
    return c * M + m, np.where(rng.random(fam.shape) < 0.04, rng.integers(0, W, fam.shape), fv), st
def mix(rng, v, q, kid, fu, fv):
    pm = np.argsort(rng.random((N, 8, W)), axis=2); inv = np.argsort(pm, axis=2)
    k = np.take_along_axis(pm, kid.reshape(N, 8, 16 * W), 2).reshape(N, 8, W, 16)
    k = np.ascontiguousarray(np.take_along_axis(k, inv[:, :, :, None], 2).transpose(0, 1, 3, 2))
    return pick(v, inv), pick(q, inv), k, np.take_along_axis(pm, fu, 2), np.take_along_axis(pm, fv, 2)
def pack(v, q, k, fu, fv, st):
    return {"vec": v.reshape(N, 128, W).astype(np.float32).astype(BF), "mark": q.reshape(N, 128, W).astype(np.float32).astype(BF), "kids": np.ascontiguousarray(k.reshape(N, 128, W)).astype(np.int32),
            "fu": np.stack([gtable(a) for a in fu]), "fv": np.stack([gtable(a) for a in fv]), "fs": np.ascontiguousarray(st).astype(np.int32)}
def setup_inputs(rng):
    v, q, kid = letters(rng, False); fu, fv, st = front(rng, False)
    return pack(*mix(rng, v, q, kid, fu, fv), st)
def setup_inputs_room(rng):
    v = np.zeros((N, 8, 16, W), np.int64); q = np.zeros((N, 8, 16, W), np.int64); k = np.zeros((N, 8, 16, W), np.int64)
    fu = np.zeros((N, 8, F), np.int64); fv = np.zeros((N, 8, F), np.int64); st = np.zeros((N, 8, F), np.int64); st[:, :, 0] = 1
    for r in range(N):
        for g in range(8):
            o = rng.permutation(W); z0 = o[2 * F]; rest = o[2 * F + 1:]
            b = rng.integers(0, 2, W); b[z0] = 0; i = int(rng.integers(0, 16))
            v[r, g] = rng.integers(0, 128, (16, 1)); v[r, g, i] += b * int(rng.integers(1, 128))
            own = rng.integers(0, N, W); w = rng.integers(0, 256, (16, W)); w[0] -= w[0] % N; w[0] += (WT @ w - own) % N; w[:, z0] = 0; q[r, g] = w
            pool = [rest[(own[rest] == a) & (b[rest] == 0)] for a in range(N)]; zero = rest[b[rest] == 0]; ones = rest[b[rest] == 1]
            pu = rng.choice(rest, 16 * F); pv = pu.copy(); mode = g if g in (2, 3) else (0, 1, 0, 4)[(r + g) % 4]
            if mode in (0, 1):
                if mode == 0:
                    n = rng.choice(np.array([0, 1, CAP - 1, CAP, CAP + 1, CAP + 8]), N)
                    if r == 0: n[1] = CAP
                    x = rng.permutation(np.concatenate([np.resize(rng.permutation(pool[a]), int(n[a])) for a in range(N)]))
                else:
                    a = rng.permutation(N)
                    x = np.concatenate([np.resize(rng.permutation(pool[a[0]]), FC - 2), np.resize(rng.permutation(pool[a[1]]), 5)])
                t = np.sort(rng.permutation(16 * F)[:len(x)])
                pu[t] = x; pv[t] = z0
            elif mode in (2, 3):
                t = int(rng.integers(0, 8))
                for n in ([LM + 1] + [LM] * (F // LM) + [1] if mode == 2 else [LM] * (F // LM - 1) + [LM - 1, 2, 1, 1]):
                    if n == 1:
                        pu[t] = rng.choice(zero); pv[t] = z0
                    else:
                        pu[t] = rng.choice(zero); pv[t] = rng.choice(ones); pu[t + n - 1] = rng.choice(ones); pv[t + n - 1] = rng.choice(zero)
                    t += n + int(rng.integers(0, 4))
            else:
                lu, lv, lx, ly = int(o[0]), int(o[F]), int(rest[0]), int(rest[1])
                j = 13 if r == 0 else 0 if r == 1 else int(rng.integers(0, 14))
                for c in (lv, lx, ly): v[r, g, :, c] = v[r, g, :, lu]
                q[r, g, j:j + 3, lu] = np.minimum(np.maximum(q[r, g, j:j + 3, lu], 2), 254)
                q[r, g, :, lx] = q[r, g, :, lu]; q[r, g, j:j + 3, lx] += np.array([1, -2, 1])
                q[r, g, :, lv] = 0; q[r, g, :, ly] = 0
                pu[0] = lu; pv[0] = lv; pu[1] = lx; pv[1] = ly
            kk = rng.choice(rest, (16, W)); kk[:, o[:F]] = pu.reshape(F, 16).T; kk[:, o[F:2 * F]] = pv.reshape(F, 16).T
            k[r, g] = kk; fu[r, g] = o[:F]; fv[r, g] = o[F:2 * F]
    return pack(v, q, k, fu, fv, st)
def swing(rng, pu, pv, t, n, low, high):
    x, y = (pu, pv) if rng.random() < 0.5 else (pv, pu)
    x[t] = rng.choice(low); y[t] = rng.choice(high); x[t + n - 1] = rng.choice(high); y[t + n - 1] = rng.choice(low)
def setup_inputs_deep(rng):
    v = np.zeros((N, 8, 16, W), np.int64); q = np.zeros((N, 8, 16, W), np.int64); k = np.zeros((N, 8, 16, W), np.int64)
    fu = np.zeros((N, 8, F), np.int64); fv = np.zeros((N, 8, F), np.int64); st = np.zeros((N, 8, F), np.int64); st[:, :, 0] = 1
    P = 16 * F; C = (LM + 15) // 16
    for r in range(N):
        for g in range(8):
            mode = (r + g) % 4; o = rng.permutation(W); z0 = int(o[2 * F]); rest = o[2 * F + 1:]
            b = rng.integers(0, 3, W) if mode > 1 else rng.integers(0, 2, W) * mode
            b[z0] = 0
            half = 8 * int(rng.integers(0, 2)); m = rng.random((16, 1)) < 0.4; m[np.arange(16) // 8 * 8 != half] = False; m[half + int(rng.integers(0, 8))] = True
            j = 8 - half + int(rng.integers(0, 6)); tri = np.zeros((16, 1), np.int64); tri[j:j + 3, 0] = int(rng.integers(1, 33)) * np.array([1, -2, 1])
            two = m.astype(np.int64) if mode == 2 else tri
            v[r, g] = np.where(m, 0, rng.integers(64, 128, (16, 1))) + 255 * m.astype(np.int64) * (b == 1) + two * (b == 2)
            own = rng.integers(0, N, W); w = rng.integers(0, 256, (16, W)); w[0] -= w[0] % N; w[0] += (WT @ w - own) % N; w[:, z0] = 0; q[r, g] = w
            pool = [rest[(own[rest] == a) & (b[rest] == 0)] for a in range(N)]; kind = [rest[b[rest] == c] for c in range(3)]
            pu = rng.choice(rest, P); pv = pu.copy(); kk = rng.choice(rest, (16, W)); a = rng.permutation(N); a0 = int(a[0]); a1 = int(a[1])
            if mode == 0:
                heads = rest[:64]; t = np.sort(rng.permutation(P)[:64]); pu[t] = heads; pv[t] = z0
                n0 = FC // 16 + (16 if g < 4 else 0)
                kk[:, z0] = z0; kk[:, heads[:n0]] = rng.choice(pool[a0], (16, n0)); kk[:, heads[n0:]] = rng.choice(pool[a1], (16, 64 - n0))
            elif mode == 1:
                t = int(rng.integers(0, 4))
                for n in range(8):
                    swing(rng, pu, pv, t, LM + 1, kind[0], kind[1]); t += LM + 1 + int(rng.integers(0, 4))
                x = np.concatenate([np.resize(rng.permutation(pool[a0]), FC - 16), np.resize(rng.permutation(pool[a1]), 20)])
                i = t + np.sort(rng.permutation(P - t)[:len(x)]); pu[i] = x; pv[i] = z0
            elif mode == 2:
                x, y = (pu, pv) if r % 2 == 0 else (pv, pu)
                t = int(rng.integers(0, 8))
                x[t:t + 257] = rng.choice(kind[1], 257); x[t + 257] = rng.choice(kind[2]); y[t:t + 258] = rng.choice(kind[0], 258); t += 258
                i = t + np.sort(rng.permutation(800)[:24]); pu[i] = rng.choice(kind[0], 24); pv[i] = z0; t += 800
                y[t:t + 257] = rng.choice(kind[1], 257); y[t + 257] = rng.choice(kind[2]); x[t:t + 258] = rng.choice(kind[0], 258); t += 258
                while t + LM + 16 < P:
                    t += int(rng.integers(0, 16)); n = int(rng.integers(2, LM + 1))
                    swing(rng, pu, pv, t, n, kind[0], kind[int(rng.integers(1, 3))]); t += n
            else:
                s = int(rng.integers(1, 6)); e = F - 4 * C
                st[r, g, s] = 1; st[r, g, e + C * np.arange(4)] = 1
                i = int(rng.integers(0, 16 * s)); pu[i] = rng.choice(kind[0]); pv[i] = rng.choice(kind[1])
                t = 16 * s
                while t + LM + 48 < 16 * e:
                    t += int(rng.integers(0, 48))
                    if rng.random() < 0.5:
                        pu[t] = rng.choice(kind[0]); pv[t] = z0; t += 1
                    else:
                        n = int(rng.integers(2, LM + 1)); swing(rng, pu, pv, t, n, kind[0], kind[2]); t += n
                for c in range(4):
                    i = 16 * (e + C * (c + 1)); x, y = (pv, pu) if c < 3 else (pu, pv)
                    x[i - LM:i] = rng.choice(kind[1], LM); y[i - LM:i] = rng.choice(kind[0], LM)
            kk[:, o[:F]] = pu.reshape(F, 16).T; kk[:, o[F:2 * F]] = pv.reshape(F, 16).T
            k[r, g] = kk; fu[r, g] = o[:F]; fv[r, g] = o[F:2 * F]
    return pack(v, q, k, fu, fv, st)
def setup_inputs_ends(rng):
    v, q, kid = letters(rng, False); fu, fv, st = front(rng, False)
    v, q, k, fu, fv = mix(rng, v, q, kid, fu, fv)
    st[:, 0] = 1; st[:, 1] = 0
    two = np.array([0, W - 1]); few = np.array([0, 1, W - 1])
    fu[:, 2] = rng.choice(two, (N, F)); fv[:, 2] = rng.choice(two, (N, F)); k[:, 2, :, 0] = rng.choice(few, (N, 16)); k[:, 2, :, W - 1] = rng.choice(few, (N, 16))
    for r in range(N):
        i = int(rng.integers(0, 16)); x = v[r, 3, i].copy(); v[r, 3] = 7; v[r, 3, i] = x
    v[:, 4] = 255 * (np.arange(W) >= W // 2); k[:, 4] = rng.integers(0, W // 2, (N, 16, W)) + (W // 2) * (np.arange(W) % 2 == 0)
    even = 2 * rng.integers(0, W // 2, (N, F)); odd = 2 * rng.integers(0, W // 2, (N, F)) + 1
    fu[:, 4] = even; fv[:, 4] = odd; fu[1::2, 4] = odd[1::2]; fv[1::2, 4] = even[1::2]; st[:, 4] = 0; st[:, 4, F - 4:] = 1
    fv[:, 5] = rng.integers(0, W, (N, F)); st[:, 5] = np.arange(F) % 3 != 1
    fv[:, 6] = fu[:, 6]; fv[:, 6, F - 1] = (fu[:, 6, F - 1] + 1 + rng.integers(0, W - 1, N)) % W
    q[:, 7] = 0; q[1::2, 7] = 255
    st[:, :, 0] = 1
    return pack(v, q, k, fu, fv, st)
def setup_inputs_alike(rng):
    v, q, kid = letters(rng, False); fu, fv, st = front(rng, False)
    v[:] = v[:1].copy(); q[:] = q[:1].copy(); kid[:] = kid[:1].copy()
    for x in (fu, fv, st):
        for r in range(1, N):
            x[r, ::2] = x[0, ::2]; x[r, 1::2] = np.roll(x[0, 1::2], r * (F // N), axis=1)
    st[:, :, 0] = 1
    return pack(*mix(rng, v, q, kid, fu, fv), st)
def setup_inputs_spread(rng):
    v, q, kid = letters(rng, True); fu, fv, st = front(rng, True)
    return pack(*mix(rng, v, q, kid, fu, fv), st)
def check_inputs(d):
    bad = []
    for k, hi in (("vec", 255), ("mark", 255), ("kids", W - 1), ("fu", W - 1), ("fv", W - 1), ("fs", 1)):
        a = np.asarray(d[k]).astype(np.float32)
        if not np.all((a >= 0) & (a <= hi) & (a == np.floor(a))): bad.append("range of " + k)
    if not np.all(np.asarray(d["fs"])[:, :, 0] == 1): bad.append("first place of fs")
    return bad
def reference(vec, mark, kids, fu, fv, fs):
    vt = vec.astype(np.float32).astype(np.int64).reshape(N, 8, 16, W); qt = mark.astype(np.float32).astype(np.int64).reshape(N, 8, 16, W); kt = kids.astype(np.int64).reshape(N, 8, 16, W)
    u = np.stack([gentries(a) for a in fu]).astype(np.int64); v = np.stack([gentries(a) for a in fv]).astype(np.int64); st = fs.astype(np.int64)
    store = np.full((N, 8, 16, TS), -1, np.int64)
    for rnd in range(RO):
        a = pick(kt, u).transpose(0, 1, 3, 2).reshape(N, 8, 16 * F); b = pick(kt, v).transpose(0, 1, 3, 2).reshape(N, 8, 16 * F)
        d = np.add.accumulate(pick(vt, a) - pick(vt, b), axis=3)
        s0 = 16 * np.repeat(np.maximum.accumulate(np.where(st == 1, np.arange(F), 0), axis=2), 16, axis=2)
        d = d - np.where((s0 > 0)[:, :, None, :], pick(d, np.maximum(s0 - 1, 0)), 0)
        last = np.zeros((N, 8, F, 16), bool); last[:, :, F - 1, 15] = True; last[:, :, :F - 1, 15] = st[:, :, 1:] == 1
        cut = np.all(d == 0, axis=2) | last.reshape(N, 8, 16 * F)
        e = np.maximum(pick(qt, a), pick(qt, b)) + d; run = np.add.accumulate(e, axis=3)
        fac = {}
        for r in range(N):
            for g in range(8):
                t1 = np.flatnonzero(cut[r, g]); t0 = np.concatenate([np.zeros(1, np.int64), t1[:-1] + 1]); ln = t1 - t0 + 1
                c = np.flatnonzero((ln <= LM) & ~((ln == 1) & (a[r, g, t0] == b[r, g, t0])))[:FC]
                t0 = t0[c]; t1 = t1[c]; ln = ln[c]
                z = (run[r, g][:, t1] - run[r, g][:, t0] + e[r, g][:, t0]) & 255
                h = (WT @ z) & (N * TS - 1)
                fac[r, g] = (t0, ln, z, h & (N - 1), h >> LB, np.zeros(len(c), bool))
        for o in range(N):
            for g in range(8):
                ix = [np.flatnonzero(fac[r, g][3] == o)[:CAP] for r in range(N)]
                zz = np.concatenate([fac[r, g][2][:, ix[r]] for r in range(N)], axis=1); pp = np.concatenate([fac[r, g][4][ix[r]] for r in range(N)])
                i = np.flatnonzero(np.any(store[o, g][:, pp] != zz, axis=0))
                win = i[np.unique(pp[i], return_index=True)[1]]
                store[o, g][:, pp[win]] = zz[:, win]
                new = np.zeros(len(pp), bool); new[win] = True; n = 0
                for r in range(N):
                    fac[r, g][5][ix[r]] = new[n:n + len(ix[r])]; n += len(ix[r])
        u = np.zeros((N, 8, F), np.int64); v = np.zeros((N, 8, F), np.int64); st = np.ones((N, 8, F), np.int64)
        for r in range(N):
            for g in range(8):
                t0, ln, z, o, p, new = fac[r, g]
                n = np.flatnonzero(new); to = np.add.accumulate(ln[n]); n = n[to <= F]; j = 0
                for x in n:
                    L = int(ln[x]); t = int(t0[x])
                    u[r, g, j:j + L] = a[r, g, t:t + L]; v[r, g, j:j + L] = b[r, g, t:t + L]; st[r, g, j + 1:j + L] = 0; j += L
    return {"yt": store.reshape(N, 128, TS).astype(np.float32).astype(BF), "yu": u.astype(np.float32), "yv": v.astype(np.float32), "ys": st.astype(np.float32)}

import numpy as np
from concourse.bass import DstId, RemoteDMATransfer
from concourse.mybir import AluOpType as A, AxisListType, ActivationFunctionType as AF

W, F, FC, CAP, TS, RO, NR = 1664, 256, 384, 48, 1024, 3, 4
P = 16 * F
NC = 4
CH = P // NC
JC = CH // 16
PE_SUB = (2,)
SL = NR * CAP
WS = (NR + 1) * FC
FR = FC // 16
INV, NEG = 1 << 22, 1 << 20

B_, F_, I_, H_, U_ = "bfloat16", "float32", "int32", "float16", "uint16"
SCRATCH = {}
for _t, _l in (
        (I_, "kid:1664 fui:16 fvi:16 fsi:256 pi:8 pm:8 zi:384 z2:384 hi:24 ow:24 hti:12 pTi:12 hri:192 pri:192 zl:384 zs:384 tq:16 tr:16 ti:256 tlo:256"),
        (U_, "lu:16 lv:16 u16:256 v16:256 l1:24 l2:24 l3:24 lo:24 pT:12 o16:12 lf:24 lb:16"),
        (H_, "boh:128 selh:2048 selmh:2048 pr1:192 th:256 mu:256 mv:256"),
        (B_, "vw:1664 mk:1664 fsb:256 dv:4096 vv:4096 sq:4096 m0:4096 m:4112 one:384 c128:384 c200:384 zz:192 bo:128 nbo:128 bo16:128 bo64k:128 bow:128 "
             "tri:128 wa:128 wb:128 wd:128 hb:128 idn:128 rg:128 sel:2048 selm:2048 sel16:2048 hsel:2048 rc:384 rTc:24 nfl:256 lastT:256 cut:260 cand:256 Bi:264 "
             "ca:384 cb:384 cc:384 zb:384 ib:100 sw:1920 ne:192 win:192 st:1232 L:384 ln:384 cu:392 al:24"),
        (F_, "qw:1664 uF:256 vF:256 eq:256 ubp:256 D:4096 qv:4096 sm:4096 sd:4096 p16:8 wc:8 r15:8 big:8 nbig:8 m500:8 w2:8 i16:16 msk:16 mw:16 rTa:24 rT:24 trS:24 "
             "trF:24 trO:12 ha:192 hc:192 thw:192 kio:256 rst:104 y:256 C:256 am:16 ac:8 bt:16 inv:24 za:384 sc:100 x1:100 x2:100 s1:50 s2:25 q0:24 dd:24 of:24 "
             "pT1:12 te:192 elT:12 od:12 oe:12 oo:12 dl:384 tz:24 tl:24 ci:24 df:24 ef:24 off:24 cf:24 tot:8 dw:640 lom:256 fil:256 nf:256 fT:16 lvf:16 luf:16 "
             "yo:256 yp:256 yq:256")):
    for _x in _l.split():
        SCRATCH[_x.split(":")[0]] = ("sbuf", [128, int(_x.split(":")[1])], _t)
OWN = "rg kid vw mk fui fvi fsi fsb sw win st yo yp yq".split()
PLACE, _w = {}, {}
for _n in list(SCRATCH):
    _t, _c = SCRATCH[_n][2], SCRATCH[_n][1][1]
    if _n not in OWN:
        _a = _w.get(_t, 0)
        PLACE[_n] = ("p" + _t, _a, _c)
        _w[_t] = _a + (_c + 15) // 16 * 16
        del SCRATCH[_n]
    else:
        PLACE[_n] = (_n, 0, _c)
for _t in _w:
    SCRATCH["p" + _t] = ("sbuf", [128, _w[_t]], _t)
SCRATCH["e3"] = ("sbuf", [128, 12, SL], B_)
for _r in range(RO):
    for _n, _c in (("K%d" % _r, SL), ("NF%d" % _r, WS)):
        SCRATCH[_n] = ("sbuf", [128, _c], B_)
        PLACE[_n] = (_n, 0, _c)
for _b in range(8):
    SCRATCH["b%d" % _b] = ("psum", [128, 512], F_)
    PLACE["b%d" % _b] = ("b%d" % _b, 0, 512)
SEMAPHORES = ["qv", "qs", "qt", "qg"] + ["d%d" % i for i in range(10)]
for _r in range(RO):
    SEMAPHORES += ["ka%d" % _r, "na%d" % _r, "kl%d" % _r, "nl%d" % _r]

MAIN = ("vv0 vv1 vv2 xm sub0 sub1 vu2 vv3 D0 xu D1 D2 sub3 sqr0 D3 qv0 qv1 qm0 reps0 qm1 sqr2 sqr1 sm0 xe sqr3 qv2 qv3 reps1 sd0 k1 "
        "qm2 qm3 k2 reps2 sm1 k3 sd1 reps3 sm2 k4 sd2 k5 sm3 k6 za sd3").split()


def rank_program(g, core, T, topo):
    rank = T.rank_of(core)
    if rank is None:
        return
    Q = {"v": g.vector, "s": g.scalar, "t": g.tensor, "g": g, "y": g.sync}
    cnt = {"v": 0, "s": 0, "t": 0, "g": 0}
    known = {e: {} for e in Q}
    recs = {}
    clocks = {}
    total = {}

    def X(n, a=0, b=None, st=1):
        n, base, width = PLACE[n]
        b = base + (width if b is None else b)
        a += base
        ap = T[n][:, a:b] if st == 1 else T[n][:, a:b:st]
        return (ap, [(n, a, b)])

    def I(n, a, b, off):
        w = X(n, a, b)
        return (w[0].indirect(off[0]), w[1] + off[1])

    def need(e, refs, write, acc=False):
        out = {}
        for (n, a, b) in refs:
            ps = n in SCRATCH and SCRATCH[n][0] == "psum"
            for (ra, rb, rw, re, ev) in recs.get(n, ()):
                over = ra < b and a < rb
                if ps and re != e:
                    hit = True
                elif not over:
                    hit = False
                elif re == e and re in cnt:
                    hit = rw and not (acc and write)
                else:
                    hit = rw or write
                if hit and out.get(ev[0], 0) < ev[1]:
                    out[ev[0]] = ev[1]
        return out

    def note(e, refs, write, ev):
        for (n, a, b) in refs:
            old = recs.get(n, [])
            if write:
                keep = [r for r in old if not (a <= r[0] and r[1] <= b)]
            else:
                keep = [r for r in old if not (r[3] == e and not r[2] and a <= r[0] and r[1] <= b)]
            keep.append((a, b, write, e, ev))
            recs[n] = keep

    def wait(e, evs):
        for s, v in sorted(evs.items()):
            if known[e].get(s, 0) >= v:
                continue
            Q[e].wait_ge(T.sem[s], v)
            known[e][s] = v
            for k, x in clocks.get((s, v), {}).items():
                if known[e].get(k, 0) < x:
                    known[e][k] = x

    def merged(e, outs, ins, acc=False):
        evs = {}
        for refs, wr in ((outs, True), (ins, False)):
            for o in refs:
                for s, v in need(e, o[1], wr, acc).items():
                    evs[s] = max(v, evs.get(s, 0))
        return evs

    def op(e, call, outs, ins, acc=False):
        wait(e, merged(e, outs, ins, acc))
        i = call()
        cnt[e] += 1
        s = "q" + e
        i.then_inc(T.sem[s], 1)
        total[s] = cnt[e]
        ev = (s, cnt[e])
        clocks[ev] = dict(known[e])
        for o in ins:
            note(e, o[1], False, ev)
        for o in outs:
            note(e, o[1], True, ev)

    def dma(e, sem, out, src, oref, iref):
        wait(e, merged(e, oref, iref))
        Q[e].dma_start(out, src).then_inc(T.sem[sem], 16)
        total[sem] = total.get(sem, 0) + 16
        ev = (sem, total[sem])
        clocks[ev] = dict(known[e])
        for o in iref:
            note("dma" + sem, o[1], False, ev)
        for o in oref:
            note("dma" + sem, o[1], True, ev)

    V = g.vector

    def tc(o, i):
        op("v", lambda: V.tensor_copy(o[0], i[0]), [o], [i])

    def tt(o, a, b, f):
        op("v", lambda: V.tensor_tensor(o[0], a[0], b[0], f), [o], [a, b])

    def ts(o, i, s1, f1, s2=None, f2=None):
        ins = [i] + [s for s in (s1, s2) if isinstance(s, tuple)]
        x1 = s1[0] if isinstance(s1, tuple) else s1
        x2 = s2[0] if isinstance(s2, tuple) else s2
        if f2 is None:
            op("v", lambda: V.tensor_scalar(o[0], i[0], x1, None, f1), [o], ins)
        else:
            op("v", lambda: V.tensor_scalar(o[0], i[0], x1, x2, f1, f2), [o], ins)

    def scan(o, a, b, init, f1, f2):
        ins = [a, b] + ([init] if isinstance(init, tuple) else [])
        x = init[0] if isinstance(init, tuple) else init
        op("v", lambda: V.tensor_tensor_scan(o[0], a[0], b[0], x, f1, f2), [o], ins)

    def total_of(o, i):
        op("v", lambda: V.tensor_reduce(o[0], i[0], AxisListType.X, A.add), [o], [i])

    def fill(o, c):
        op("v", lambda: V.memset(o[0], c), [o], [])

    def scat(o, i):
        op("v", lambda: V.tensor_copy(o[0], i[0]), [(None, o[1][:1])], [i, (None, o[1][1:])])

    def act(o, i, f=AF.Identity, **kw):
        ref = [(None, x[1]) for x in kw.values() if isinstance(x, tuple)]
        kw = {k: x[0] if isinstance(x, tuple) else x for k, x in kw.items()}
        op("s", lambda: g.scalar.activation(o[0], i[0], f, **kw), [o], [i] + ref)

    def mm(o, l, r, start=True, stop=True):
        op("t", lambda: g.tensor.matmul(o[0], l[0], r[0], start, stop), [o], [l, r], acc=not start)

    def selmm(o, m, src, base, n, start=True, stop=True):
        for i in range(16):
            mm(o, X(m, 128 * i, 128 * i + 128), X(src, base + i, base + 16 * n, 16), start and i == 0, stop and i == 15)

    def iota(o, pattern, base, cm, small=True):
        if small:
            op("g", lambda: g.iota(o[0], pattern, base, cm, allow_small_or_imprecise_dtypes=True), [o], [])
        else:
            op("g", lambda: g.iota(o[0], pattern, base, cm), [o], [])

    def asel(o, i, pattern, cmp, fl, base, cm):
        op("g", lambda: g.affine_select(o[0], i[0], pattern, cmp, fl, base, cm), [o], [i])

    def send(src, sstep, dst, dstep, lsem, rsem):
        s = (None, [(src, sstep * d, sstep * d + CAP) for d in range(NR) if d != rank])
        wait("g", merged("g", [], [s]))
        tr, n = [], 0
        for x, d in enumerate(r for r in range(NR) if r != rank):
            eng = topo.engines(core, T.cores[d])[2 * x:2 * x + 2]
            rid, pid = topo.addr(T.cores[d], core)
            tr.append(RemoteDMATransfer(dst_ids=[DstId(rid=rid, pnc=pid)], dma_engine_mask=sum(1 << e for e in eng), remote_sem=T.sem[rsem],
                                        src=T[src][:, sstep * d:sstep * d + CAP], dst=T[dst][:, dstep * rank:dstep * rank + CAP]))
            n += len(eng)
        g.remote_dma_fused(tr, local_sem=T.sem[lsem])
        total[lsem] = n
        total[rsem] = n
        note("rem" + lsem, s[1], False, (lsem, n))
        for d in range(NR):
            if d != rank:
                note("arr", [(dst, dstep * d, dstep * d + CAP)], True, (rsem, n))

    dma("s", "d0", T.fvi[:], T.fv[:], [X("fvi")], [])
    dma("y", "d1", T.kid[:], T.kids[:], [X("kid")], [])
    dma("s", "d2", T.fui[:], T.fu[:], [X("fui")], [])
    dma("s", "d3", T.fsi[0:8, :], T.fs[:], [X("fsi")], [])
    dma("y", "d4", T.vw[:], T.vec[:], [X("vw")], [])
    dma("y", "d5", T.mk[:], T.mark[:], [X("mk")], [])
    blk = [[-16, 8], [0, 16]]
    blk2 = [[16, 8], [0, 16]]
    o128 = X("one", 0, 128)

    def block(n, src=None):
        asel(X(n), src or X(n), blk, A.is_ge, 0.0, 0, 1)
        asel(X(n), X(n), blk2, A.is_ge, 0.0, 15, -1)
    fill(X("one"), 1.0)
    fill(X("sel"), 0.0)
    iota(X("pi", 0, 1), [[0, 1]], 0, 1, False)
    block("bo", o128)
    asel(X("rg"), o128, [[1, 128]], A.is_ge, 0.0, 0, -16)
    asel(X("rg"), X("rg"), [[-1, 128]], A.is_ge, 0.0, 15, 16)
    asel(X("idn"), o128, [[-1, 128]], A.is_equal, 0.0, 0, 1)
    asel(X("wa"), o128, [[1, 128]], A.is_ge, 0.0, -1, -1)
    asel(X("wa"), X("wa"), [[1, 128]], A.not_equal, 128.0, -1, -1)
    asel(X("wa"), X("wa"), [[1, 128]], A.not_equal, -256.0, 0, -1)
    block("wa")
    asel(X("wb"), o128, [[-1, 128]], A.not_equal, 128.0, -15, 1)
    block("wb")
    asel(X("wd"), X("bo"), [[-1, 128]], A.is_ge, 0.0, 0, 1)
    asel(X("tri"), X("bo"), [[1, 128]], A.is_ge, 0.0, 0, -1)
    iota(X("i16"), [[1, 16]], 0, 0)
    iota(X("rTa"), [[16, FR]], 0, 0)
    iota(X("rc"), [[1, FC]], -192, 0)
    iota(X("kio"), [[1, F]], 0, 0)
    ts(X("pm", 0, 1), X("pi", 0, 1), 15, A.bitwise_and)
    tc(X("p16", 0, 1), X("pm", 0, 1))
    p16 = X("p16", 0, 1)
    ts(X("wc", 0, 1), p16, -14.0, A.mult, 255.0, A.add)
    ts(X("r15", 0, 1), p16, 15.0, A.is_equal)
    ts(X("big", 0, 1), X("r15", 0, 1), 1e20, A.mult)
    ts(X("nbig", 0, 1), X("r15", 0, 1), -1e20, A.mult)
    fill(X("cut", 0, 4), 0.0)
    tc(X("cut", 3, 4), X("r15", 0, 1))
    for i in range(16):
        tc(X("sel", 128 * i + i, 128 * i + 128, 16), X("bo", i, 128, 16))
    act(X("selm"), X("sel"), scale=0.0625)
    act(X("sel16"), X("sel"), scale=16.0)
    act(X("hsel"), X("sel"), scale=X("wc", 0, 1))
    fill(X("m0"), 1.0)
    tc(X("lv"), X("fvi"))
    tc(X("lu"), X("fui"))
    op("v", lambda: V.tensor_copy(T.fsb[0:8, :], T.fsi[0:8, :]), [X("fsb")], [X("fsi")])
    op("t", lambda: g.tensor.matmul(T.b5[:, 0:F], T.rg[0:8, :], T.fsb[0:8, :], True, True), [X("b5", 0, F)], [X("rg"), X("fsb")])
    ts(X("nfl"), X("b5", 0, F), -1.0, A.mult, 1.0, A.add)
    tc(X("lastT", F - 1, F), X("big", 0, 1))
    ts(X("bo16"), X("bo"), 16.0, A.mult)
    ts(X("nbo"), X("bo"), -1.0, A.mult)
    fill(X("m", 0, 1), 0.0)
    fill(X("m500"), -500.0)
    fill(X("Bi", 0, 1), -192.0)
    fill(X("c200"), 200.0)
    fill(X("c128"), -128.0)
    for o in range(NR):
        fill(X("sw", FC * o, FC * o + CAP), -1.0)

    def later():
        fill(X("st"), -1.0)
        fill(X("zz"), 0.0)
        ts(X("hb"), X("bo"), X("wc", 0, 1), A.mult)
        ts(X("trO"), X("rT", 0, 12), float(TS + 16), A.add)
        fill(X("ha"), 0.5)
        fill(X("ha", 0, SL, 16), 0.0)
        fill(X("hc"), 0.0)
        fill(X("hc", 0, SL, 16), 65536.0)
        scan(X("thw"), X("ha"), X("hc"), 0.0, A.mult, A.add)
        tt(X("mw"), X("thw", 0, 16), X("msk"), A.mult)
        total_of(X("w2", 0, 1), X("mw"))
        ts(X("bow"), X("bo"), X("w2", 0, 1), A.mult, 0.5, A.mult)
        ts(X("bo64k"), X("bo"), 65536.0, A.mult)

    def later2():
        ts(X("trF"), X("rT"), float(F - 128), A.add)
        fill(X("cu", 0, 1), -128.0)
        tc(X("selmh"), X("selm"))
        tc(X("selh"), X("sel"))
        tc(X("boh"), X("bo"))

    def ch(n, c):
        return X(n, c * CH, c * CH + CH)

    def lst(n, c):
        return X(n, c * JC, c * JC + JC)

    def halves(c):
        return [(h, c * CH + 512 * h) for h in range(CH // 512)]

    def vv(c):
        act(ch("vv", c), I("vw", 0, W, lst("v16", c)), scale=-1.0)

    def vu(c):
        act(ch("dv", c), I("vw", 0, W, lst("u16", c)))
        for h, a in halves(c):
            mm(X("b%d" % h), X("idn"), X("dv", a, a + 512), True, False)
            mm(X("b%d" % h), X("idn"), X("vv", a, a + 512), False, True)

    def sub(c):
        tt(ch("dv", c), I("vw", 0, W, lst("u16", c)), ch("vv", c), A.add)

    def dscan(c):
        if c in PE_SUB:
            for h, a in halves(c):
                scan(X("D", a, a + 512), X("m0", a, a + 512), X("b%d" % h), X("D", a - 1, a) if a else 0.0, A.mult, A.add)
        else:
            a = c * CH
            scan(ch("D", c), ch("m0", c), ch("dv", c), X("D", a - 1, a) if a else 0.0, A.mult, A.add)

    def sqr(c):
        act(ch("sq", c), ch("D", c), AF.Square)
        selmm(X("b4", c * JC, c * JC + JC), "sel", "sq", c * CH, JC)

    def reps(c):
        for h, a in halves(c):
            mm(X("b%d" % (2 + h)), X("bo"), X("sq", a, a + 512), True, False)
            mm(X("b%d" % (2 + h), 15, 512, 16), X("nbo"), X("lastT", a // 16, a // 16 + 32), False, True)
        for h, a in halves(c):
            act(X("m", a + 1, a + 513), X("b%d" % (2 + h)), AF.Sigmoid, bias=X("m500", 0, 1), scale=1000.0)

    def qv(c):
        act(ch("qv", c), I("qw", 0, W, lst("v16", c)))

    def qm(c):
        tt(ch("qv", c), I("qw", 0, W, lst("u16", c)), ch("qv", c), A.max)

    def sums(n, src, c):
        a = c * CH
        scan(ch(n, c), ch("m", c), ch(src, c), X(n, a - 1, a) if a else 0.0, A.mult, A.add)

    def k1():
        tt(X("cut", 4, F + 4), X("b4", 0, F), X("lastT"), A.is_le)
        mm(X("b5", 0, F), X("bo16"), X("one", 0, F), True, False)
        for x, (n, d) in enumerate((("bo", 1), ("bo", 2), ("wd", 0), ("wb", 3), ("wa", 4))):
            mm(X("b5", 0, F), X(n), X("cut", d, d + F), False, x == 4)

    def k2():
        tt(X("y"), X("b5", 0, F), X("ubp"), A.is_lt)
        tt(X("cand"), X("b5", 0, F), X("y"), A.min)
        mm(X("b6", 256, 512), X("bo"), X("cand"))
        mm(X("b6", 0, 256), X("tri"), X("cand"))

    def k3():
        scan(X("Bi", 1, F + 1), X("b6", 256, 512), X("c200", 0, F), -192.0, A.add, A.min)
        tt(X("am"), X("Bi", 16, F + 1, 16), X("msk"), A.mult)
        total_of(X("ac", 0, 1), X("am"))
        ts(X("ca"), X("rc"), X("ac", 0, 1), A.is_ge, 16.0, A.mult)
        tt(X("C"), X("b6", 0, 256), X("Bi", 0, F), A.add)
        selmm(X("b5", 0, 16), "selm", "Bi", 1, 16)
        selmm(X("b7", 0, FR), "selm", "ca", 0, FR)
        ts(X("inv"), X("rTc"), X("Bi", F, F + 1), A.is_ge, float(INV), A.mult)

    def k4():
        tc(X("bt"), X("b5", 0, 16))
        ts(X("l1"), X("b7", 0, FR), 15.0, A.min)
        tt(X("cb"), I("bt", 0, 16, X("l1")), X("rc"), A.is_le)
        selmm(X("b4", 0, FR), "sel", "ca", 0, FR, True, False)
        selmm(X("b4", 0, FR), "sel", "cb", 0, FR, False, True)
        selmm(X("b6", 0, FR), "sel16", "ca", 0, FR, True, False)
        selmm(X("b6", 0, FR), "sel16", "cb", 0, FR, False, False)

    def k5():
        ts(X("l2"), X("b4", 0, FR), 255.0, A.min)
        tt(X("cc"), I("C", 0, F, X("l2")), X("rc"), A.is_le)
        selmm(X("b6", 0, FR), "sel", "cc", 0, FR, False, True)
        for x, (n, r) in enumerate((("bo16", "ca"), ("bo16", "cb"), ("bo", "cc"), ("bo", "c128"), ("idn", "one"))):
            mm(X("b7", 0, FC), X(n), X(r), x == 0, x == 4)

    def k6():
        ts(X("l3"), X("b6", 0, FR), float(P - 1), A.min)

    def xm():
        tc(X("m0", 0, P, 16), X("nfl"))
        ts(X("lastT", 0, F - 1), X("nfl", 1, F), X("nbig", 0, 1), A.mult, X("big", 0, 1), A.add)

    def xu():
        tc(X("uF"), X("u16"))
        tc(X("vF"), X("v16"))

    def xe():
        tt(X("eq"), X("uF"), X("vF"), A.is_equal)
        ts(X("ubp"), X("eq"), -72.0, A.mult, 200.0, A.add)

    def za():
        act(X("za"), I("sm", 0, P, X("l3")))

    steps = {"vv": vv, "vu": vu, "sub": sub, "D": dscan, "sqr": sqr, "reps": reps, "qv": qv, "qm": qm,
             "sm": lambda c: sums("sm", "qv", c), "sd": lambda c: sums("sd", "D", c)}
    whole = {"k1": k1, "k2": k2, "k3": k3, "k4": k4, "k5": k5, "k6": k6, "xm": xm, "xu": xu, "xe": xe, "za": za}

    for rnd in range(RO):
        K, NF, lastr = "K%d" % rnd, "NF%d" % rnd, rnd == RO - 1
        if rnd == 0:
            tc(X("v16"), I("kid", 0, W, X("lv")))
        tc(X("u16"), I("kid", 0, W, X("lu")))
        if rnd > 0:
            ts(X("fil"), X("kio"), X("tot", 0, 1), A.is_lt)
            tt(X("nfl"), X("nf"), X("fil"), A.mult)
        for s in MAIN:
            if s == "qv0" and rnd == 0:
                act(X("qw"), X("mk"), bias=32768.0)
                ts(X("msk"), X("i16"), p16, A.is_equal)
                ts(X("rT"), X("rTa"), p16, A.add)
                ts(X("rTc"), X("rT"), -192.0, A.add)
                ts(X("trS"), X("rT"), float(NR * FC), A.add)
                fill(X("x1", 0, 1), 0.0)
                fill(X("rst"), 1.0)
                fill(X("rst", 0, 100, 25), 0.0)
                fill(X("ib"), 0.0)
            if s in whole:
                whole[s]()
            else:
                steps[s[:-1]](int(s[-1]))
        tt(X("zi"), I("sd", 0, P, X("l3")), X("za"), A.add)
        ts(X("z2"), X("zi"), 255, A.bitwise_and)
        tc(X("zb"), X("z2"))
        selmm(X("b5", 0, FR), "hsel", "zb", 0, FR)
        tt(X("hi"), X("b5", 0, FR), X("inv"), A.add)
        ts(X("ow"), X("hi"), INV + 3, A.bitwise_and)
        for o in range(NR):
            ts(X("ib", 25 * o + 1, 25 * o + 25), X("ow"), float(o), A.is_equal)
        mm(X("b6", 256, 356), X("bo"), X("ib"))
        mm(X("b6", 0, 100), X("tri"), X("ib"))
        ts(X("q0"), X("ow"), float(FC), A.mult, -1.0, A.add)
        scan(X("sc"), X("rst", 0, 100), X("b6", 256, 356), 0.0, A.mult, A.add)
        tt(X("x1", 1, 100), X("b6", 1, 100), X("sc", 0, 99), A.add)
        tt(X("x2"), X("x1"), X("ib"), A.mult)
        tt(X("s1"), X("x2", 0, 50), X("x2", 50, 100), A.add)
        tt(X("s2"), X("s1", 0, 25), X("s1", 25, 50), A.add)
        tt(X("dd"), X("s2", 1, 25), X("q0"), A.add)
        tt(X("of"), X("dd"), X("trS"), A.min)
        tc(X("lo"), X("of"))
        scat(I("sw", 0, WS, X("lo")), X("zb"))
        send("sw", FC, K, CAP, "kl%d" % rnd, "ka%d" % rnd)
        own = (CAP * rank, CAP * rank + CAP)
        strip = (FC * rank, FC * rank + CAP)
        tc(X(K, own[0], own[1]), X("sw", strip[0], strip[1]))
        if rnd == 0:
            later()
        tc(X("zl"), X("za"))
        ts(X("zs"), X("zl"), 15, A.arith_shift_right)
        tc(X("L"), X("zs"))
        fill(X("dw"), -5000.0)
        selmm(X("b5", 0, 12), "hsel", K, 0, 12)
        mm(X("b0", 0, SL), X("hb"), X(K))
        mm(X("b6", 0, SL), X("bo64k"), X("zz"), True, False)
        tc(X("hti"), X("b5", 0, 12))
        ts(X("pTi"), X("hti"), 2, A.arith_shift_right, NEG + TS - 1, A.bitwise_and)
        ts(X("pT"), X("pTi"), float(TS), A.min)
        tt(X("ne"), I("st", 0, TS + 16, X("pT")), X(K), A.not_equal)
        selmm(X("b4", 0, 12), "sel", "ne", 0, 12)
        mm(X("b1", 0, SL), X("bo64k"), X("ne"))
        tc(X("hri"), X("b0", 0, SL))
        ts(X("pri"), X("hri"), 2, A.arith_shift_right, TS - 1, A.bitwise_and)
        tc(X("pr1"), X("pri"))
        tc(X("pT1"), X("pTi"))
        ts(X("elT"), X("b4", 0, 12), 0.5, A.is_ge)
        for c in range(12):
            n = SL - 16 * c
            op("v", lambda c=c, n=n: V.tensor_scalar(T.e3[:, c, 0:n], X("pr1", 16 * c, SL)[0], X("pT1", c, c + 1)[0], X("elT", c, c + 1)[0], A.is_equal, A.mult),
               [(None, [("e3", c * SL, c * SL + n)])], [X("pr1", 16 * c, SL), X("pT1", c, c + 1), X("elT", c, c + 1)])
        tt(X("te"), X("b1", 0, SL), X("thw"), A.min)
        for c in range(12):
            if c < 11:
                op("t", lambda c=c: g.tensor.matmul(T.b6[:, 16 * c + 16:SL], X("bo64k")[0], T.e3[:, c, 16:SL - 16 * c], False, False),
                   [X("b6", 16 * c + 16, SL)], [X("bo64k"), (None, [("e3", c * SL + 16, c * SL + SL - 16 * c)])], acc=True)
            op("t", lambda c=c: g.tensor.matmul(T.b6[:, 16 * c:16 * c + 16], X("bow")[0], T.e3[:, c, 0:16], False, c == 11),
               [X("b6", 16 * c, 16 * c + 16)], [X("bow"), (None, [("e3", c * SL, c * SL + 16)])], acc=True)
        tt(X("win"), X("b6", 0, SL), X("te"), A.is_lt)
        send("win", CAP, NF, FC, "nl%d" % rnd, "na%d" % rnd)
        tc(X(NF, strip[0], strip[1]), X("win", own[0], own[1]))
        for o in range(NR):
            fill(X(NF, FC * o + CAP, FC * (o + 1) if o < NR - 1 else WS), 0.0)
        if rnd == 0:
            later2()
        selmm(X("b4", 0, 12), "selm", "win", 0, 12)
        if not lastr:
            for o in range(NR):
                fill(X("sw", FC * o, FC * o + CAP), -1.0)
        tt(X("od"), X("pTi"), X("trO"), A.subtract)
        tt(X("oe"), X("b4", 0, 12), X("od"), A.mult)
        tt(X("oo"), X("oe"), X("trO"), A.add)
        tc(X("o16"), X("oo"))
        scat(I("st", 0, TS + 16 + SL, X("o16")), X(K))
        if lastr:
            dma("y", "d6", T.yt[:], T.st[:, 0:TS], [], [X("st", 0, TS)])
        tt(X("ln"), I(NF, 0, WS, X("lo")), X("L"), A.mult)
        selmm(X("b4", 0, FR), "selm", "ln", 0, FR)
        scan(X("cu", 1, FC + 1), X("ln"), X("c200"), -128.0, A.add, A.min)
        selmm(X("b5", 0, FR), "selm", "cu", 1, FR)
        tt(X("dl"), X("b7", 0, FC), X("ln"), A.subtract)
        ts(X("tz"), X("b4", 0, FR), 0.5, A.is_lt, -4096.0, A.mult)
        tt(X("tl"), X("b4", 0, FR), X("tz"), A.add)
        ts(X("ci"), X("b5", 0, FR), 128.5, A.is_gt, 4096.0, A.mult)
        tt(X("df"), X("b5", 0, FR), X("tl"), A.subtract)
        tt(X("ef"), X("df"), X("ci"), A.add)
        tt(X("off"), X("ef"), X("trF"), A.min)
        ts(X("lf"), X("off"), 128.0, A.add)
        scat(I("dw", 0, F + FC, X("lf")), X("dl"))
        scan(X("th"), X("one", 0, F), X("dw", 0, F), -5000.0, A.add, A.max)
        selmm(X("b5", 0, 16), "selmh", "th", 0, 16)
        tc(X("ti"), X("th"))
        ts(X("cf"), X("off"), 127.5, A.is_lt)
        ts(X("tlo"), X("ti"), 15, A.bitwise_and)
        tt(X("al"), X("b4", 0, FR), X("cf"), A.mult)
        mm(X("b6", 0, FR), X("bo"), X("al"))
        ts(X("lom"), X("tlo"), p16, A.is_equal)
        ts(X("tq"), X("b5", 0, 16), 2048.0, A.add)
        ts(X("tr"), X("tq"), 4, A.arith_shift_right, 255, A.bitwise_and)
        tc(X("lb"), X("tr"))
        tt(X("mv"), I("vF", 0, F, X("lb")), X("lom"), A.mult)
        if not lastr:
            selmm(X("b4", 0, 16), "selh", "mv", 0, 16)
        else:
            mm(X("b4", 0, F), X("boh"), X("mv"))
        tt(X("mu"), I("uF", 0, F, X("lb")), X("lom"), A.mult)
        total_of(X("tot", 0, 1), X("b6", 0, FR))
        ts(X("nf"), X("dw", 0, F), -4000.0, A.is_le)
        if not lastr:
            selmm(X("b5", 0, 16), "selh", "mu", 0, 16)
            ts(X("fT"), X("rT", 0, 16), X("tot", 0, 1), A.is_lt)
            tt(X("lvf"), X("b4", 0, 16), X("fT"), A.mult)
            tc(X("lv"), X("lvf"))
            tc(X("v16"), I("kid", 0, W, X("lv")))
            tt(X("luf"), X("b5", 0, 16), X("fT"), A.mult)
            tc(X("lu"), X("luf"))
        else:
            mm(X("b5", 0, F), X("boh"), X("mu"))
            ts(X("fil"), X("kio"), X("tot", 0, 1), A.is_lt)
            tt(X("yp"), X("b4", 0, F), X("fil"), A.mult)
            dma("y", "d8", T.yv[:], T.yp[0:128:16, :], [], [X("yp")])
            tt(X("yo"), X("b5", 0, F), X("fil"), A.mult)
            dma("s", "d7", T.yu[:], T.yo[0:128:16, :], [], [X("yo")])
            tt(X("nf"), X("nf"), X("fil"), A.mult)
            ts(X("yq"), X("nf"), -1.0, A.mult, 1.0, A.add)
            dma("y", "d9", T.ys[:], T.yq[0:128:16, :], [], [X("yq")])
    known["g"].clear()
    wait("g", total)
